import numpy as np
import ml_dtypes


def mxq(x, axis, fmt="e4m3"):
    dtype, down = {"e4m3": (ml_dtypes.float8_e4m3fn, 7), "e5m2": (ml_dtypes.float8_e5m2, 14)}[fmt]
    v = np.moveaxis(np.asarray(x, np.float32).astype(ml_dtypes.bfloat16).astype(np.float64), axis, -1)
    blocks = v.reshape(v.shape[:-1] + (-1, 32))
    amax = np.abs(blocks).max(-1, keepdims=True)
    byte = np.maximum(np.where(amax > 0, np.frexp(amax)[1] - 1 + 127, 0) - down, 1)
    scale = np.exp2(byte - 127.0)
    codes = (blocks / scale).astype(np.float32).astype(dtype).astype(np.float64)
    return np.moveaxis((codes * scale).reshape(v.shape), -1, axis)


WIDE = False


def mx_kscale(k):
    if not WIDE:
        return np.ones(k)
    levels = np.array([10, -10, 5, -5, 0])
    if k % 512:
        return np.exp2(np.random.permutation(np.resize(levels, k // 32))).repeat(32)
    a = np.empty((k // 512, 16))
    for p in range(k // 512):
        a[p, :8] = np.random.permutation(np.resize(levels, 8))
        for g in range(8):
            far = levels[np.abs(levels - a[p, g]) >= 10]
            a[p, g + 8] = far[np.random.randint(len(far))]
    return np.exp2(a.ravel()).repeat(32)


def f64(x):
    return np.asarray(x).astype(np.float64)


def striped(idx):
    return np.tile(np.asarray(idx).reshape(-1, 16).T, (8, 1)).astype(np.uint16)


def unstriped(offs):
    return offs[:16].T.reshape(-1).astype(np.int64)


def striped8(idx):
    return np.asarray(idx).reshape(8, -1, 16).transpose(0, 2, 1).reshape(128, -1).astype(np.uint16)


def unstriped8(offs):
    return offs.reshape(8, 16, -1).transpose(0, 2, 1).reshape(8, -1).astype(np.int64)


def pick8(x, idx, run):
    r = np.arange(len(x))
    return x[r[:, None], idx[r % (8 * run) // run]]


E2M1 = np.array([0.0, 0.5, 1.0, 1.5, 2.0, 3.0, 4.0, 6.0, -0.0, -0.5, -1.0, -1.5, -2.0, -3.0, -4.0, -6.0])


def pack_weight(w, fmt):
    k, n = w.shape
    w = f64(np.asarray(w, np.float32).astype(ml_dtypes.bfloat16)).reshape(k // 32, 32, n)
    amax = np.abs(w).max(1)
    if fmt == "e4m3":
        byte = np.frexp(amax)[1] - 1 + 127 - 7
    else:
        mant, ex = np.frexp(amax / 6.0)
        byte = np.where(mant > 0.5, ex, ex - 1) + 127
    byte = np.clip(np.where(amax > 0, byte, 1), 1, 254)
    scaled = (w * np.exp2(127.0 - byte)[:, None, :]).reshape(k, n).astype(np.float32)
    by_word = np.ascontiguousarray(scaled.reshape(k // 512, 128, 4, n).transpose(0, 1, 3, 2))
    if fmt == "e4m3":
        words = by_word.astype(ml_dtypes.float8_e4m3fn).view(np.uint8)
    else:
        c = by_word.astype(ml_dtypes.float4_e2m1fn).view(np.uint8) & 0xF
        words = (c[..., 0::2] | (c[..., 1::2] << 4)).reshape(k // 512, 128, 2 * n)
    return np.ascontiguousarray(words), np.ascontiguousarray(byte.astype(np.uint8).reshape(k // 512, 16, n))


def unpack_weight(words, scales, fmt):
    g, _, n = scales.shape
    words = np.ascontiguousarray(words).reshape(g, 128, n, -1)
    if fmt == "e4m3":
        vals = words.view(ml_dtypes.float8_e4m3fn).astype(np.float64)
    else:
        nib = np.empty((g, 128, n, 4), np.uint8)
        nib[..., 0::2] = words & 0xF
        nib[..., 1::2] = words >> 4
        vals = E2M1[nib]
    vals = vals * np.repeat(np.exp2(scales.astype(np.float64) - 127.0), 8, axis=1)[..., None]
    return vals.transpose(0, 1, 3, 2).reshape(g * 512, n)


D, T, U, I, Q = 512, 2048, 256, 1024, 128


def setup_inputs():
    n = np.random.standard_normal
    idx = np.stack([np.random.permutation(T)[:I] for _ in range(8)])
    idx2 = np.random.randint(0, U, I)
    fd = mx_kscale(D)
    piecep = pack_weight(n((D, T)) / fd[:, None], "e4m3")
    return {
        "hid": (n((D, Q)) * 1.0 / np.sqrt(D) * fd[:, None]).astype(np.float32),
        "piece_words": piecep[0],
        "piece_scales": piecep[1],
        "fam": (n((D, U)) * 0.7 / fd[:, None]).astype(np.float32),
        "bias": (np.random.uniform(-0.5, 0.5, (1, I))).astype(np.float32),
        "offs": striped8(idx),
        "offs2": striped(idx2),
    }


def reference(hid, piece_words, piece_scales, fam, bias, offs, offs2):
    idx = unstriped8(offs)
    idx2 = unstriped(offs2)
    pieceu = unpack_weight(piece_words, piece_scales, "e4m3")
    hidq = mxq(f64(hid), 0, "e4m3")
    pieceidxg = pick8(pieceu, idx, 64)
    a = hidq.T @ pieceidxg
    famq = mxq(f64(fam), 0, "e4m3")
    b = hidq.T @ famq
    s = a + b[:, idx2] + f64(bias)
    r = s - np.max(s, axis=1, keepdims=True)
    y = r - np.log(np.sum(np.exp(r), axis=1, keepdims=True))
    return y

@@ -1,0 +1,142 @@
+import math
+from contextlib import ExitStack
+
+import concourse.mybir as mybir
+from concourse.masks import make_identity
+
+F32 = mybir.dt.float32
+BF16 = mybir.dt.bfloat16
+I32 = mybir.dt.int32
+U32 = mybir.dt.uint32
+U16 = mybir.dt.uint16
+U8 = mybir.dt.uint8
+FP8X4 = mybir.dt.float8_e4m3fn_x4
+ALU = mybir.AluOpType
+ACT = mybir.ActivationFunctionType
+AXIS = mybir.AxisListType
+
+P = 128
+PACK = 4
+T, U, I, Q = 2048, 256, 1024, 128
+HALF = 512
+B_WINDOW = 544
+NODES = 88
+STEP = 0.375
+FIRST = -29.25
+
+FLOPS = 2 * 512 * Q * (I + U)
+
+
+def tile_attend_composedvocab_kernel(tc, hid, piece_words, piece_scales, fam, bias, offs, offs2, out):
+    nc = tc.nc
+    with ExitStack() as ctx:
+        sb = ctx.enter_context(tc.tile_pool(name="sb", bufs=1))
+        ps = ctx.enter_context(tc.psum_pool(name="ps", bufs=1))
+
+        piece_list = sb.tile([P, I // 16], U16, name="piece_list")
+        family_list = sb.tile([P, I // 16], U16, name="family_list")
+        scale_store = sb.tile([P, T], U8, name="scale_store", align_bytes=64)
+        word_store = sb.tile([P, T], U32, name="word_store", align_bytes=64)
+        hid_raw = sb.tile([P, PACK, Q], F32, name="hid_raw")
+        fam_raw = sb.tile([P, PACK, U], F32, name="fam_raw")
+        bias_col = sb.tile([P, 8], F32, name="bias_col")
+
+        nc.vector.memset(scale_store[:].bitcast(I32), 0)
+        nc.sync.dma_start(out=scale_store[0:P:8, :].bitcast(I32), in_=piece_scales[0].bitcast(I32))
+        nc.sync.dma_start(piece_list[:], offs)
+        nc.sync.dma_start(out=bias_col[:], in_=bias.rearrange("o (p c) -> (o p) c", c=8))
+        nc.sync.dma_start(family_list[:], offs2)
+        nc.sync.dma_start(out=word_store[:].bitcast(I32),
+                          in_=piece_words[0].rearrange("p n t -> p (n t)").bitcast(I32))
+        nc.sync.dma_start(out=hid_raw[:], in_=hid.rearrange("(p j) q -> p j q", j=PACK))
+        nc.sync.dma_start(out=fam_raw[:], in_=fam.rearrange("(p j) u -> p j u", j=PACK))
+
+        piece_plane = sb.tile([P, I], U8, name="piece_plane", align_bytes=64)
+        nc.vector.memset(piece_plane[:].bitcast(I32), 0)
+        b_table = sb.tile([P, B_WINDOW], F32, name="b_table")
+        nc.vector.memset(b_table[:, U:], 0.0)
+
+        counts = sb.tile([P, NODES], F32, name="counts")
+        ident = sb.tile([P, P], F32, name="ident")
+        nc.vector.memset(ident[:], 0.0)
+        make_identity(nc, ident[:], nomemset=True)
+        ones = sb.tile([P, NODES], F32, name="ones")
+        nc.vector.memset(ones[:], 1.0)
+        nc.vector.tensor_tensor_scan(out=counts[:], data0=ones[:], data1=ones[:], initial=-1.0,
+                                     op0=ALU.mult, op1=ALU.add)
+        nodes = sb.tile([P, NODES], F32, name="nodes")
+        nc.scalar.activation(out=nodes[:], in_=counts[:], func=ACT.Exp, scale=STEP, bias=FIRST)
+        neg_nodes = sb.tile([P, NODES], F32, name="neg_nodes")
+        nc.scalar.activation(out=neg_nodes[:], in_=nodes[:], func=ACT.Copy, scale=-1.0)
+        terms = sb.tile([P, NODES], F32, name="terms")
+        s_one = sb.tile([P, 1], F32, name="s_one")
+        nc.scalar.activation(out=terms[:], in_=neg_nodes[:], func=ACT.Exp, bias=math.log(STEP), accum_out=s_one[:])
+
+        scale_got = sb.tile([P, I], U8, name="scale_got", align_bytes=64)
+        nc.vector.tensor_copy(out=scale_got[:], in_=scale_store[:].indirect(piece_list[:]))
+        for j in range(4):
+            nc.sync.dma_start(out=piece_plane[j:P:32, :].bitcast(I32), in_=scale_got[8 * j:P:32, :].bitcast(I32))
+
+        hid_bf = sb.tile([P, Q, PACK], BF16, name="hid_bf", align_bytes=64)
+        nc.scalar.copy(out=hid_bf[:], in_=hid_raw[:].rearrange("p j q -> p q j"))
+        hid_codes = sb.tile([P, Q], U32, name="hid_codes", align_bytes=64)
+        hid_plane = sb.tile([P, Q], U8, name="hid_plane", align_bytes=64)
+        nc.vector.quantize_mx(out=hid_codes[:].bitcast(FP8X4), scales=hid_plane[:],
+                              in_=hid_bf[:].rearrange("p q j -> p (q j)"))
+
+        bias_rows = sb.tile([P, P, 8], F32, name="bias_rows")
+        for g in range(2):
+            bank = ps.tile([P, 4, P], F32, name=f"bias_bank{g}")
+            for c in range(4):
+                col = 4 * g + c
+                nc.tensor.transpose(bank[:, c, :], bias_col[:, col:col + 1].to_broadcast([P, P]), ident[:])
+            nc.scalar.copy(out=bias_rows[:, :, 4 * g:4 * g + 4], in_=bank[:].rearrange("q c p -> q p c"))
+        bias_flat = bias_rows[:].rearrange("q p c -> q (p c)")
+
+        a_banks = []
+        for h in range(2):
+            words = sb.tile([P, HALF], U32, name=f"words{h}", align_bytes=64)
+            nc.vector.tensor_copy(out=words[:], in_=word_store[:].indirect(piece_list[:, 32 * h:32 * (h + 1)]))
+            a_bank = ps.tile([P, HALF], F32, name=f"a_bank{h}")
+            nc.tensor.matmul_mx(out=a_bank[:], lhsT=hid_codes[:].bitcast(FP8X4), lhsT_scale=hid_plane[:],
+                                rhs=words[:].bitcast(FP8X4), rhs_scale=piece_plane[:, HALF * h:HALF * (h + 1)],
+                                start=True, stop=True)
+            a_banks.append(a_bank)
+
+        fam_bf = sb.tile([P, U, PACK], BF16, name="fam_bf", align_bytes=64)
+        nc.scalar.copy(out=fam_bf[:], in_=fam_raw[:].rearrange("p j u -> p u j"))
+        fam_codes = sb.tile([P, U], U32, name="fam_codes", align_bytes=64)
+        fam_plane = sb.tile([P, U], U8, name="fam_plane", align_bytes=64)
+        nc.vector.quantize_mx(out=fam_codes[:].bitcast(FP8X4), scales=fam_plane[:],
+                              in_=fam_bf[:].rearrange("p u j -> p (u j)"))
+        b_bank = ps.tile([P, U], F32, name="b_bank")
+        nc.tensor.matmul_mx(out=b_bank[:], lhsT=hid_codes[:].bitcast(FP8X4), lhsT_scale=hid_plane[:],
+                            rhs=fam_codes[:].bitcast(FP8X4), rhs_scale=fam_plane[:], start=True, stop=True)
+        nc.scalar.copy(out=b_table[:, :U], in_=b_bank[:])
+
+        partial = fam_raw[:].rearrange("p j u -> p (j u)")
+        for h in range(2):
+            cols = slice(HALF * h, HALF * (h + 1))
+            nc.vector.tensor_tensor(out=partial[:, cols], in0=a_banks[h][:], in1=bias_flat[:, cols], op=ALU.add)
+        score = sb.tile([P, I], F32, name="score")
+        for h in range(2):
+            cols = slice(HALF * h, HALF * (h + 1))
+            nc.vector.tensor_tensor(out=score[:, cols], in0=b_table[:].indirect(family_list[:, 32 * h:32 * (h + 1)]),
+                                    in1=partial[:, cols], op=ALU.add)
+        neg_max = sb.tile([P, 1], F32, name="neg_max")
+        nc.vector.tensor_reduce(out=neg_max[:], in_=score[:], axis=AXIS.X, op=ALU.max, negate=True)
+        weights = sb.tile([P, I], F32, name="weights")
+        total = sb.tile([P, 1], F32, name="total")
+        nc.scalar.activation(out=weights[:], in_=score[:], func=ACT.Exp, bias=neg_max[:], accum_out=total[:])
+        shift = sb.tile([P, 1], F32, name="shift")
+        nc.vector.tensor_tensor(out=shift[:], in0=neg_max[:], in1=s_one[:], op=ALU.subtract)
+        terms2 = sb.tile([P, NODES], F32, name="terms2")
+        s_total = sb.tile([P, 1], F32, name="s_total")
+        nc.scalar.activation(out=terms2[:], in_=neg_nodes[:], func=ACT.Exp, scale=total[:], bias=math.log(STEP),
+                             accum_out=s_total[:])
+        result = sb.tile([P, I], F32, name="result")
+        for h, queue in enumerate((nc.sync, nc.scalar)):
+            cols = slice(HALF * h, HALF * (h + 1))
+            nc.vector.tensor_scalar(out=result[:, cols], in0=score[:, cols], scalar1=shift[:], scalar2=s_total[:],
+                                    op0=ALU.add, op1=ALU.add)
+            queue.dma_start(out=out[:, cols], in_=result[:, cols])

@@ -44,22 +44,22 @@ def tile_attend_composedvocab_kernel(tc, hid, piece_words, piece_scales, fam, bi
         nc.vector.memset(scale_store[:].bitcast(I32), 0)
         nc.sync.dma_start(out=scale_store[0:P:8, :].bitcast(I32), in_=piece_scales[0].bitcast(I32))
         nc.sync.dma_start(piece_list[:], offs)
+        nc.sync.dma_start(out=hid_raw[:], in_=hid.rearrange("(p j) q -> p j q", j=PACK))
         nc.sync.dma_start(out=bias_col[:], in_=bias.rearrange("o (p c) -> (o p) c", c=8))
         nc.sync.dma_start(family_list[:], offs2)
+        nc.sync.dma_start(out=fam_raw[:], in_=fam.rearrange("(p j) u -> p j u", j=PACK))
         nc.sync.dma_start(out=word_store[:].bitcast(I32),
                           in_=piece_words[0].rearrange("p n t -> p (n t)").bitcast(I32))
-        nc.sync.dma_start(out=hid_raw[:], in_=hid.rearrange("(p j) q -> p j q", j=PACK))
-        nc.sync.dma_start(out=fam_raw[:], in_=fam.rearrange("(p j) u -> p j u", j=PACK))
 
+        ident = sb.tile([P, P], F32, name="ident")
+        nc.vector.memset(ident[:], 0.0)
+        make_identity(nc, ident[:], nomemset=True)
         piece_plane = sb.tile([P, I], U8, name="piece_plane", align_bytes=64)
         nc.vector.memset(piece_plane[:].bitcast(I32), 0)
         b_table = sb.tile([P, B_WINDOW], F32, name="b_table")
         nc.vector.memset(b_table[:, U:], 0.0)
 
         counts = sb.tile([P, NODES], F32, name="counts")
-        ident = sb.tile([P, P], F32, name="ident")
-        nc.vector.memset(ident[:], 0.0)
-        make_identity(nc, ident[:], nomemset=True)
         ones = sb.tile([P, NODES], F32, name="ones")
         nc.vector.memset(ones[:], 1.0)
         nc.vector.tensor_tensor_scan(out=counts[:], data0=ones[:], data1=ones[:], initial=-1.0,
@@ -71,6 +71,15 @@ def tile_attend_composedvocab_kernel(tc, hid, piece_words, piece_scales, fam, bi
         terms = sb.tile([P, NODES], F32, name="terms")
         s_one = sb.tile([P, 1], F32, name="s_one")
         nc.scalar.activation(out=terms[:], in_=neg_nodes[:], func=ACT.Exp, bias=math.log(STEP), accum_out=s_one[:])
+
+        bias_rows = sb.tile([P, P, 8], F32, name="bias_rows")
+        for g in range(2):
+            bank = ps.tile([P, 4, P], F32, name=f"bias_bank{g}")
+            for c in range(4):
+                col = 4 * g + c
+                nc.tensor.transpose(bank[:, c, :], bias_col[:, col:col + 1].to_broadcast([P, P]), ident[:])
+            nc.scalar.copy(out=bias_rows[:, :, 4 * g:4 * g + 4], in_=bank[:].rearrange("q c p -> q p c"))
+        bias_flat = bias_rows[:].rearrange("q p c -> q (p c)")
 
         scale_got = sb.tile([P, I], U8, name="scale_got", align_bytes=64)
         nc.vector.tensor_copy(out=scale_got[:], in_=scale_store[:].indirect(piece_list[:]))
@@ -84,25 +93,6 @@ def tile_attend_composedvocab_kernel(tc, hid, piece_words, piece_scales, fam, bi
         nc.vector.quantize_mx(out=hid_codes[:].bitcast(FP8X4), scales=hid_plane[:],
                               in_=hid_bf[:].rearrange("p q j -> p (q j)"))
 
-        bias_rows = sb.tile([P, P, 8], F32, name="bias_rows")
-        for g in range(2):
-            bank = ps.tile([P, 4, P], F32, name=f"bias_bank{g}")
-            for c in range(4):
-                col = 4 * g + c
-                nc.tensor.transpose(bank[:, c, :], bias_col[:, col:col + 1].to_broadcast([P, P]), ident[:])
-            nc.scalar.copy(out=bias_rows[:, :, 4 * g:4 * g + 4], in_=bank[:].rearrange("q c p -> q p c"))
-        bias_flat = bias_rows[:].rearrange("q p c -> q (p c)")
-
-        a_banks = []
-        for h in range(2):
-            words = sb.tile([P, HALF], U32, name=f"words{h}", align_bytes=64)
-            nc.vector.tensor_copy(out=words[:], in_=word_store[:].indirect(piece_list[:, 32 * h:32 * (h + 1)]))
-            a_bank = ps.tile([P, HALF], F32, name=f"a_bank{h}")
-            nc.tensor.matmul_mx(out=a_bank[:], lhsT=hid_codes[:].bitcast(FP8X4), lhsT_scale=hid_plane[:],
-                                rhs=words[:].bitcast(FP8X4), rhs_scale=piece_plane[:, HALF * h:HALF * (h + 1)],
-                                start=True, stop=True)
-            a_banks.append(a_bank)
-
         fam_bf = sb.tile([P, U, PACK], BF16, name="fam_bf", align_bytes=64)
         nc.scalar.copy(out=fam_bf[:], in_=fam_raw[:].rearrange("p j u -> p u j"))
         fam_codes = sb.tile([P, U], U32, name="fam_codes", align_bytes=64)
@@ -114,29 +104,60 @@ def tile_attend_composedvocab_kernel(tc, hid, piece_words, piece_scales, fam, bi
                             rhs=fam_codes[:].bitcast(FP8X4), rhs_scale=fam_plane[:], start=True, stop=True)
         nc.scalar.copy(out=b_table[:, :U], in_=b_bank[:])
 
-        partial = fam_raw[:].rearrange("p j u -> p (j u)")
+        a_banks = []
         for h in range(2):
+            words = sb.tile([P, HALF], U32, name=f"words{h}", align_bytes=64)
+            nc.vector.tensor_copy(out=words[:], in_=word_store[:].indirect(piece_list[:, 32 * h:32 * (h + 1)]))
+            a_bank = ps.tile([P, HALF], F32, name=f"a_bank{h}")
+            nc.tensor.matmul_mx(out=a_bank[:], lhsT=hid_codes[:].bitcast(FP8X4), lhsT_scale=hid_plane[:],
+                                rhs=words[:].bitcast(FP8X4), rhs_scale=piece_plane[:, HALF * h:HALF * (h + 1)],
+                                start=True, stop=True)
+            a_banks.append(a_bank)
+
+        looked = sb.tile([P, I], F32, name="looked")
+        score = sb.tile([P, I + 8], F32, name="score")
+        weights = sb.tile([P, HALF + 8], F32, name="weights")
+        terms2 = sb.tile([P, NODES], F32, name="terms2")
+
+        def look_up(lo, hi):
+            nc.vector.tensor_tensor(out=looked[:, lo:hi], in0=b_table[:].indirect(family_list[:, lo // 16:hi // 16]),
+                                    in1=bias_flat[:, lo:hi], op=ALU.add)
+
+        def add_pieces(h):
             cols = slice(HALF * h, HALF * (h + 1))
-            nc.vector.tensor_tensor(out=partial[:, cols], in0=a_banks[h][:], in1=bias_flat[:, cols], op=ALU.add)
-        score = sb.tile([P, I], F32, name="score")
-        for h in range(2):
-            cols = slice(HALF * h, HALF * (h + 1))
-            nc.vector.tensor_tensor(out=score[:, cols], in0=b_table[:].indirect(family_list[:, 32 * h:32 * (h + 1)]),
-                                    in1=partial[:, cols], op=ALU.add)
+            nc.vector.tensor_tensor(out=score[:, cols], in0=a_banks[h][:], in1=looked[:, cols], op=ALU.add)
+
+        look_up(0, HALF)
+        add_pieces(0)
+        neg_max0 = sb.tile([P, 1], F32, name="neg_max0")
+        nc.vector.tensor_reduce(out=neg_max0[:], in_=score[:, :HALF], axis=AXIS.X, op=ALU.max, negate=True)
+        total0 = sb.tile([P, 1], F32, name="total0")
+        nc.scalar.activation(out=weights[:, :HALF], in_=score[:, :HALF], func=ACT.Exp, bias=neg_max0[:], accum_out=total0[:])
+        base0 = sb.tile([P, 1], F32, name="base0")
+        nc.scalar.activation(out=base0[:], in_=neg_max0[:], func=ACT.Identity, scale=-1.0, bias=s_one[:])
+        s_total0 = sb.tile([P, 1], F32, name="s_total0")
+        nc.scalar.activation(out=terms2[:], in_=neg_nodes[:], func=ACT.Exp, scale=total0[:], bias=math.log(STEP),
+                             accum_out=s_total0[:])
+        nc.scalar.activation(out=score[:, I:I + 1], in_=s_total0[:], func=ACT.Identity, scale=-1.0, bias=base0[:])
+
+        look_up(HALF, HALF + 256)
+        look_up(HALF + 256, I)
+        add_pieces(1)
         neg_max = sb.tile([P, 1], F32, name="neg_max")
-        nc.vector.tensor_reduce(out=neg_max[:], in_=score[:], axis=AXIS.X, op=ALU.max, negate=True)
-        weights = sb.tile([P, I], F32, name="weights")
+        negated = sb.tile([P, HALF], F32, name="negated")
+        nc.vector.tensor_scalar(out=negated[:], in0=score[:, HALF:I], scalar1=-1.0, scalar2=neg_max0[:],
+                                op0=ALU.mult, op1=ALU.min, accum_out=neg_max[:])
         total = sb.tile([P, 1], F32, name="total")
-        nc.scalar.activation(out=weights[:], in_=score[:], func=ACT.Exp, bias=neg_max[:], accum_out=total[:])
+        nc.scalar.activation(out=weights[:, :HALF + 1], in_=score[:, HALF:I + 1], func=ACT.Exp, bias=neg_max[:],
+                             accum_out=total[:])
         shift = sb.tile([P, 1], F32, name="shift")
         nc.vector.tensor_tensor(out=shift[:], in0=neg_max[:], in1=s_one[:], op=ALU.subtract)
-        terms2 = sb.tile([P, NODES], F32, name="terms2")
         s_total = sb.tile([P, 1], F32, name="s_total")
         nc.scalar.activation(out=terms2[:], in_=neg_nodes[:], func=ACT.Exp, scale=total[:], bias=math.log(STEP),
                              accum_out=s_total[:])
         result = sb.tile([P, I], F32, name="result")
-        for h, queue in enumerate((nc.sync, nc.scalar)):
-            cols = slice(HALF * h, HALF * (h + 1))
+        for lo, hi, queue in ((0, 256, nc.sync), (256, 640, nc.scalar), (640, I, nc.sync)):
+            cols = slice(lo, hi)
             nc.vector.tensor_scalar(out=result[:, cols], in0=score[:, cols], scalar1=shift[:], scalar2=s_total[:],
                                     op0=ALU.add, op1=ALU.add)
             queue.dma_start(out=out[:, cols], in_=result[:, cols])

@@ -17,14 +17,19 @@ AXIS = mybir.AxisListType
 
 P = 128
 PACK = 4
-T, U, I, Q = 2048, 256, 1024, 128
+D, T, U, I, Q = 512, 2048, 256, 1024, 128
+GROUP = 16
+QUADRANT = 32
+BLOCK_ROWS = 8
 HALF = 512
-B_WINDOW = 544
-NODES = 88
-STEP = 0.375
-FIRST = -29.25
+QUARTER = 256
+BIAS_RUN = I // P
+PER_BANK = HALF // P
+B_TABLE = HALF + 32
+NODES, STEP, FIRST = 88, 0.375, -29.25
+STORE_EDGES = (0, 256, 640, I)
 
-FLOPS = 2 * 512 * Q * (I + U)
+FLOPS = 2 * D * Q * (I + U)
 
 
 def tile_attend_composedvocab_kernel(tc, hid, piece_words, piece_scales, fam, bias, offs, offs2, out):
@@ -33,30 +38,30 @@ def tile_attend_composedvocab_kernel(tc, hid, piece_words, piece_scales, fam, bi
         sb = ctx.enter_context(tc.tile_pool(name="sb", bufs=1))
         ps = ctx.enter_context(tc.psum_pool(name="ps", bufs=1))
 
-        piece_list = sb.tile([P, I // 16], U16, name="piece_list")
-        family_list = sb.tile([P, I // 16], U16, name="family_list")
+        piece_list = sb.tile([P, I // GROUP], U16, name="piece_list")
+        family_list = sb.tile([P, I // GROUP], U16, name="family_list")
         scale_store = sb.tile([P, T], U8, name="scale_store", align_bytes=64)
         word_store = sb.tile([P, T], U32, name="word_store", align_bytes=64)
         hid_raw = sb.tile([P, PACK, Q], F32, name="hid_raw")
         fam_raw = sb.tile([P, PACK, U], F32, name="fam_raw")
-        bias_col = sb.tile([P, 8], F32, name="bias_col")
+        bias_runs = sb.tile([P, BIAS_RUN], F32, name="bias_runs")
 
         nc.vector.memset(scale_store[:].bitcast(I32), 0)
-        nc.sync.dma_start(out=scale_store[0:P:8, :].bitcast(I32), in_=piece_scales[0].bitcast(I32))
+        nc.sync.dma_start(out=scale_store[0:P:BLOCK_ROWS, :].bitcast(I32), in_=piece_scales[0].bitcast(I32))
         nc.sync.dma_start(piece_list[:], offs)
+        nc.sync.dma_start(out=bias_runs[:], in_=bias.rearrange("o (p c) -> (o p) c", c=BIAS_RUN))
         nc.sync.dma_start(out=hid_raw[:], in_=hid.rearrange("(p j) q -> p j q", j=PACK))
-        nc.sync.dma_start(out=bias_col[:], in_=bias.rearrange("o (p c) -> (o p) c", c=8))
         nc.sync.dma_start(family_list[:], offs2)
-        nc.sync.dma_start(out=fam_raw[:], in_=fam.rearrange("(p j) u -> p j u", j=PACK))
         nc.sync.dma_start(out=word_store[:].bitcast(I32),
                           in_=piece_words[0].rearrange("p n t -> p (n t)").bitcast(I32))
+        nc.sync.dma_start(out=fam_raw[:], in_=fam.rearrange("(p j) u -> p j u", j=PACK))
 
         ident = sb.tile([P, P], F32, name="ident")
         nc.vector.memset(ident[:], 0.0)
         make_identity(nc, ident[:], nomemset=True)
-        piece_plane = sb.tile([P, I], U8, name="piece_plane", align_bytes=64)
-        nc.vector.memset(piece_plane[:].bitcast(I32), 0)
-        b_table = sb.tile([P, B_WINDOW], F32, name="b_table")
+        planes = sb.tile([P, I], U8, name="planes", align_bytes=64)
+        nc.vector.memset(planes[:].bitcast(I32), 0)
+        b_table = sb.tile([P, B_TABLE], F32, name="b_table")
         nc.vector.memset(b_table[:, U:], 0.0)
 
         counts = sb.tile([P, NODES], F32, name="counts")
@@ -68,81 +73,98 @@ def tile_attend_composedvocab_kernel(tc, hid, piece_words, piece_scales, fam, bi
         nc.scalar.activation(out=nodes[:], in_=counts[:], func=ACT.Exp, scale=STEP, bias=FIRST)
         neg_nodes = sb.tile([P, NODES], F32, name="neg_nodes")
         nc.scalar.activation(out=neg_nodes[:], in_=nodes[:], func=ACT.Copy, scale=-1.0)
-        terms = sb.tile([P, NODES], F32, name="terms")
-        s_one = sb.tile([P, 1], F32, name="s_one")
-        nc.scalar.activation(out=terms[:], in_=neg_nodes[:], func=ACT.Exp, bias=math.log(STEP), accum_out=s_one[:])
 
-        bias_rows = sb.tile([P, P, 8], F32, name="bias_rows")
-        for g in range(2):
-            bank = ps.tile([P, 4, P], F32, name=f"bias_bank{g}")
-            for c in range(4):
-                col = 4 * g + c
-                nc.tensor.transpose(bank[:, c, :], bias_col[:, col:col + 1].to_broadcast([P, P]), ident[:])
-            nc.scalar.copy(out=bias_rows[:, :, 4 * g:4 * g + 4], in_=bank[:].rearrange("q c p -> q p c"))
+        def node_sum(terms, total, result):
+            nc.scalar.activation(out=terms[:], in_=neg_nodes[:], func=ACT.Exp, scale=total,
+                                 bias=math.log(STEP), accum_out=result[:])
+
+        terms_one = sb.tile([P, NODES], F32, name="terms_one")
+        sum_one = sb.tile([P, 1], F32, name="sum_one")
+        node_sum(terms_one, 1.0, sum_one)
+
+        bias_rows = sb.tile([P, P, BIAS_RUN], F32, name="bias_rows")
+        for g in range(BIAS_RUN // PER_BANK):
+            bank = ps.tile([P, PER_BANK, P], F32, name=f"bias_bank{g}")
+            for c in range(PER_BANK):
+                col = PER_BANK * g + c
+                nc.tensor.transpose(bank[:, c, :], bias_runs[:, col:col + 1].to_broadcast([P, P]), ident[:])
+            nc.scalar.copy(out=bias_rows[:, :, PER_BANK * g:PER_BANK * (g + 1)],
+                           in_=bank[:].rearrange("q c p -> q p c"))
         bias_flat = bias_rows[:].rearrange("q p c -> q (p c)")
 
         scale_got = sb.tile([P, I], U8, name="scale_got", align_bytes=64)
         nc.vector.tensor_copy(out=scale_got[:], in_=scale_store[:].indirect(piece_list[:]))
-        for j in range(4):
-            nc.sync.dma_start(out=piece_plane[j:P:32, :].bitcast(I32), in_=scale_got[8 * j:P:32, :].bitcast(I32))
+        for j in range(QUADRANT // BLOCK_ROWS):
+            queue = (nc.sync, nc.scalar)[j % 2]
+            queue.dma_start(out=planes[j:P:QUADRANT, :].bitcast(I32),
+                            in_=scale_got[BLOCK_ROWS * j:P:QUADRANT, :].bitcast(I32))
+
+        def round_and_interleave(grouped, raw):
+            nc.scalar.copy(out=grouped[:].rearrange("p (c i) j -> p c j i", i=4),
+                           in_=raw[:].rearrange("p j (c i) -> p c j i", i=4))
 
         hid_bf = sb.tile([P, Q, PACK], BF16, name="hid_bf", align_bytes=64)
-        nc.scalar.copy(out=hid_bf[:], in_=hid_raw[:].rearrange("p j q -> p q j"))
+        round_and_interleave(hid_bf, hid_raw)
         hid_codes = sb.tile([P, Q], U32, name="hid_codes", align_bytes=64)
         hid_plane = sb.tile([P, Q], U8, name="hid_plane", align_bytes=64)
         nc.vector.quantize_mx(out=hid_codes[:].bitcast(FP8X4), scales=hid_plane[:],
                               in_=hid_bf[:].rearrange("p q j -> p (q j)"))
 
-        fam_bf = sb.tile([P, U, PACK], BF16, name="fam_bf", align_bytes=64)
-        nc.scalar.copy(out=fam_bf[:], in_=fam_raw[:].rearrange("p j u -> p u j"))
-        fam_codes = sb.tile([P, U], U32, name="fam_codes", align_bytes=64)
-        fam_plane = sb.tile([P, U], U8, name="fam_plane", align_bytes=64)
-        nc.vector.quantize_mx(out=fam_codes[:].bitcast(FP8X4), scales=fam_plane[:],
-                              in_=fam_bf[:].rearrange("p u j -> p (u j)"))
-        b_bank = ps.tile([P, U], F32, name="b_bank")
-        nc.tensor.matmul_mx(out=b_bank[:], lhsT=hid_codes[:].bitcast(FP8X4), lhsT_scale=hid_plane[:],
-                            rhs=fam_codes[:].bitcast(FP8X4), rhs_scale=fam_plane[:], start=True, stop=True)
-        nc.scalar.copy(out=b_table[:, :U], in_=b_bank[:])
+        def list_slice(offsets, lo, hi):
+            return offsets[:, lo // GROUP:hi // GROUP]
 
-        a_banks = []
+        word_halves = []
         for h in range(2):
             words = sb.tile([P, HALF], U32, name=f"words{h}", align_bytes=64)
-            nc.vector.tensor_copy(out=words[:], in_=word_store[:].indirect(piece_list[:, 32 * h:32 * (h + 1)]))
-            a_bank = ps.tile([P, HALF], F32, name=f"a_bank{h}")
-            nc.tensor.matmul_mx(out=a_bank[:], lhsT=hid_codes[:].bitcast(FP8X4), lhsT_scale=hid_plane[:],
-                                rhs=words[:].bitcast(FP8X4), rhs_scale=piece_plane[:, HALF * h:HALF * (h + 1)],
-                                start=True, stop=True)
-            a_banks.append(a_bank)
+            nc.vector.tensor_copy(out=words[:],
+                                  in_=word_store[:].indirect(list_slice(piece_list, HALF * h, HALF * (h + 1))))
+            word_halves.append(words)
+        a_banks = [ps.tile([P, HALF], F32, name=f"a_bank{h}") for h in range(2)]
 
-        looked = sb.tile([P, I], F32, name="looked")
+        def times_hid(acc, codes, plane):
+            nc.tensor.matmul_mx(out=acc, lhsT=hid_codes[:].bitcast(FP8X4), lhsT_scale=hid_plane[:],
+                                rhs=codes.bitcast(FP8X4), rhs_scale=plane, start=True, stop=True)
+
+        for h, lo, hi in ((0, 0, QUARTER), (0, QUARTER, HALF), (1, 0, HALF)):
+            times_hid(a_banks[h][:, lo:hi], word_halves[h][:, lo:hi], planes[:, HALF * h + lo:HALF * h + hi])
+
+        fam_bf = sb.tile([P, U, PACK], BF16, name="fam_bf", align_bytes=64)
+        round_and_interleave(fam_bf, fam_raw)
+        fam_codes = sb.tile([P, U], U32, name="fam_codes", align_bytes=64)
+        fam_plane = planes[4:P, :U]
+        nc.vector.quantize_mx(out=fam_codes[:].bitcast(FP8X4), scales=fam_plane,
+                              in_=fam_bf[:].rearrange("p u j -> p (u j)"))
+        b_bank = ps.tile([P, U], F32, name="b_bank")
+        times_hid(b_bank[:], fam_codes[:], fam_plane)
+        nc.scalar.copy(out=b_table[:, :U], in_=b_bank[:])
+
+        partial = fam_raw[:].rearrange("p j u -> p (j u)")
         score = sb.tile([P, I + 8], F32, name="score")
         weights = sb.tile([P, HALF + 8], F32, name="weights")
-        terms2 = sb.tile([P, NODES], F32, name="terms2")
+        terms = sb.tile([P, NODES], F32, name="terms")
 
-        def look_up(lo, hi):
-            nc.vector.tensor_tensor(out=looked[:, lo:hi], in0=b_table[:].indirect(family_list[:, lo // 16:hi // 16]),
-                                    in1=bias_flat[:, lo:hi], op=ALU.add)
+        def add_family(lo, hi):
+            nc.vector.tensor_tensor(out=score[:, lo:hi], in0=b_table[:].indirect(list_slice(family_list, lo, hi)),
+                                    in1=partial[:, lo:hi], op=ALU.add)
 
-        def add_pieces(h):
+        for h in range(2):
             cols = slice(HALF * h, HALF * (h + 1))
-            nc.vector.tensor_tensor(out=score[:, cols], in0=a_banks[h][:], in1=looked[:, cols], op=ALU.add)
+            nc.vector.tensor_tensor(out=partial[:, cols], in0=a_banks[h][:], in1=bias_flat[:, cols], op=ALU.add)
 
-        look_up(0, HALF)
-        add_pieces(0)
+        add_family(0, HALF)
         neg_max0 = sb.tile([P, 1], F32, name="neg_max0")
         nc.vector.tensor_reduce(out=neg_max0[:], in_=score[:, :HALF], axis=AXIS.X, op=ALU.max, negate=True)
         total0 = sb.tile([P, 1], F32, name="total0")
-        nc.scalar.activation(out=weights[:, :HALF], in_=score[:, :HALF], func=ACT.Exp, bias=neg_max0[:], accum_out=total0[:])
+        nc.scalar.activation(out=weights[:, :HALF], in_=score[:, :HALF], func=ACT.Exp, bias=neg_max0[:],
+                             accum_out=total0[:])
         base0 = sb.tile([P, 1], F32, name="base0")
-        nc.scalar.activation(out=base0[:], in_=neg_max0[:], func=ACT.Identity, scale=-1.0, bias=s_one[:])
-        s_total0 = sb.tile([P, 1], F32, name="s_total0")
-        nc.scalar.activation(out=terms2[:], in_=neg_nodes[:], func=ACT.Exp, scale=total0[:], bias=math.log(STEP),
-                             accum_out=s_total0[:])
-        nc.scalar.activation(out=score[:, I:I + 1], in_=s_total0[:], func=ACT.Identity, scale=-1.0, bias=base0[:])
+        nc.scalar.activation(out=base0[:], in_=neg_max0[:], func=ACT.Identity, scale=-1.0, bias=sum_one[:])
+        sum0 = sb.tile([P, 1], F32, name="sum0")
+        node_sum(terms, total0[:], sum0)
+        nc.scalar.activation(out=score[:, I:I + 1], in_=sum0[:], func=ACT.Identity, scale=-1.0, bias=base0[:])
 
-        look_up(HALF, HALF + 256)
-        look_up(HALF + 256, I)
-        add_pieces(1)
+        add_family(HALF, HALF + QUARTER)
+        add_family(HALF + QUARTER, I)
         neg_max = sb.tile([P, 1], F32, name="neg_max")
         negated = sb.tile([P, HALF], F32, name="negated")
         nc.vector.tensor_scalar(out=negated[:], in0=score[:, HALF:I], scalar1=-1.0, scalar2=neg_max0[:],
@@ -151,13 +173,13 @@ def tile_attend_composedvocab_kernel(tc, hid, piece_words, piece_scales, fam, bi
         nc.scalar.activation(out=weights[:, :HALF + 1], in_=score[:, HALF:I + 1], func=ACT.Exp, bias=neg_max[:],
                              accum_out=total[:])
         shift = sb.tile([P, 1], F32, name="shift")
-        nc.vector.tensor_tensor(out=shift[:], in0=neg_max[:], in1=s_one[:], op=ALU.subtract)
-        s_total = sb.tile([P, 1], F32, name="s_total")
-        nc.scalar.activation(out=terms2[:], in_=neg_nodes[:], func=ACT.Exp, scale=total[:], bias=math.log(STEP),
-                             accum_out=s_total[:])
+        nc.vector.tensor_tensor(out=shift[:], in0=neg_max[:], in1=sum_one[:], op=ALU.subtract)
+        sum_all = sb.tile([P, 1], F32, name="sum_all")
+        node_sum(terms, total[:], sum_all)
+
         result = sb.tile([P, I], F32, name="result")
-        for lo, hi, queue in ((0, 256, nc.sync), (256, 640, nc.scalar), (640, I, nc.sync)):
-            cols = slice(lo, hi)
-            nc.vector.tensor_scalar(out=result[:, cols], in0=score[:, cols], scalar1=shift[:], scalar2=s_total[:],
+        for k in range(len(STORE_EDGES) - 1):
+            cols = slice(STORE_EDGES[k], STORE_EDGES[k + 1])
+            nc.vector.tensor_scalar(out=result[:, cols], in0=score[:, cols], scalar1=shift[:], scalar2=sum_all[:],
                                     op0=ALU.add, op1=ALU.add)
-            queue.dma_start(out=out[:, cols], in_=result[:, cols])
+            (nc.sync, nc.scalar)[k % 2].dma_start(out=out[:, cols], in_=result[:, cols])

import math
from contextlib import ExitStack

import concourse.mybir as mybir
from concourse.masks import make_identity

F32 = mybir.dt.float32
BF16 = mybir.dt.bfloat16
I32 = mybir.dt.int32
U32 = mybir.dt.uint32
U16 = mybir.dt.uint16
U8 = mybir.dt.uint8
FP8X4 = mybir.dt.float8_e4m3fn_x4
ALU = mybir.AluOpType
ACT = mybir.ActivationFunctionType
AXIS = mybir.AxisListType

P = 128
PACK = 4
D, T, U, I, Q = 512, 2048, 256, 1024, 128
GROUP = 16
QUADRANT = 32
BLOCK_ROWS = 8
HALF = 512
QUARTER = 256
BIAS_RUN = I // P
PER_BANK = HALF // P
B_TABLE = HALF + 32
NODES, STEP, FIRST = 88, 0.375, -29.25
STORE_EDGES = (0, 256, 640, I)

FLOPS = 2 * D * Q * (I + U)


def tile_attend_composedvocab_kernel(tc, hid, piece_words, piece_scales, fam, bias, offs, offs2, out):
    nc = tc.nc
    with ExitStack() as ctx:
        sb = ctx.enter_context(tc.tile_pool(name="sb", bufs=1))
        ps = ctx.enter_context(tc.psum_pool(name="ps", bufs=1))

        piece_list = sb.tile([P, I // GROUP], U16, name="piece_list")
        family_list = sb.tile([P, I // GROUP], U16, name="family_list")
        scale_store = sb.tile([P, T], U8, name="scale_store", align_bytes=64)
        word_store = sb.tile([P, T], U32, name="word_store", align_bytes=64)
        hid_raw = sb.tile([P, PACK, Q], F32, name="hid_raw")
        fam_raw = sb.tile([P, PACK, U], F32, name="fam_raw")
        bias_runs = sb.tile([P, BIAS_RUN], F32, name="bias_runs")

        nc.vector.memset(scale_store[:].bitcast(I32), 0)
        nc.sync.dma_start(out=scale_store[0:P:BLOCK_ROWS, :].bitcast(I32), in_=piece_scales[0].bitcast(I32))
        nc.sync.dma_start(piece_list[:], offs)
        nc.sync.dma_start(out=bias_runs[:], in_=bias.rearrange("o (p c) -> (o p) c", c=BIAS_RUN))
        nc.sync.dma_start(out=hid_raw[:], in_=hid.rearrange("(p j) q -> p j q", j=PACK))
        nc.sync.dma_start(family_list[:], offs2)
        nc.sync.dma_start(out=word_store[:].bitcast(I32),
                          in_=piece_words[0].rearrange("p n t -> p (n t)").bitcast(I32))
        nc.sync.dma_start(out=fam_raw[:], in_=fam.rearrange("(p j) u -> p j u", j=PACK))

        ident = sb.tile([P, P], F32, name="ident")
        nc.vector.memset(ident[:], 0.0)
        make_identity(nc, ident[:], nomemset=True)
        planes = sb.tile([P, I], U8, name="planes", align_bytes=64)
        nc.vector.memset(planes[:].bitcast(I32), 0)
        b_table = sb.tile([P, B_TABLE], F32, name="b_table")
        nc.vector.memset(b_table[:, U:], 0.0)

        counts = sb.tile([P, NODES], F32, name="counts")
        ones = sb.tile([P, NODES], F32, name="ones")
        nc.vector.memset(ones[:], 1.0)
        nc.vector.tensor_tensor_scan(out=counts[:], data0=ones[:], data1=ones[:], initial=-1.0,
                                     op0=ALU.mult, op1=ALU.add)
        nodes = sb.tile([P, NODES], F32, name="nodes")
        nc.scalar.activation(out=nodes[:], in_=counts[:], func=ACT.Exp, scale=STEP, bias=FIRST)
        neg_nodes = sb.tile([P, NODES], F32, name="neg_nodes")
        nc.scalar.activation(out=neg_nodes[:], in_=nodes[:], func=ACT.Copy, scale=-1.0)

        def node_sum(terms, total, result):
            nc.scalar.activation(out=terms[:], in_=neg_nodes[:], func=ACT.Exp, scale=total,
                                 bias=math.log(STEP), accum_out=result[:])

        terms_one = sb.tile([P, NODES], F32, name="terms_one")
        sum_one = sb.tile([P, 1], F32, name="sum_one")
        node_sum(terms_one, 1.0, sum_one)

        bias_rows = sb.tile([P, P, BIAS_RUN], F32, name="bias_rows")
        for g in range(BIAS_RUN // PER_BANK):
            bank = ps.tile([P, PER_BANK, P], F32, name=f"bias_bank{g}")
            for c in range(PER_BANK):
                col = PER_BANK * g + c
                nc.tensor.transpose(bank[:, c, :], bias_runs[:, col:col + 1].to_broadcast([P, P]), ident[:])
            nc.scalar.copy(out=bias_rows[:, :, PER_BANK * g:PER_BANK * (g + 1)],
                           in_=bank[:].rearrange("q c p -> q p c"))
        bias_flat = bias_rows[:].rearrange("q p c -> q (p c)")

        scale_got = sb.tile([P, I], U8, name="scale_got", align_bytes=64)
        nc.vector.tensor_copy(out=scale_got[:], in_=scale_store[:].indirect(piece_list[:]))
        for j in range(QUADRANT // BLOCK_ROWS):
            queue = (nc.sync, nc.scalar)[j % 2]
            queue.dma_start(out=planes[j:P:QUADRANT, :].bitcast(I32),
                            in_=scale_got[BLOCK_ROWS * j:P:QUADRANT, :].bitcast(I32))

        def round_and_interleave(grouped, raw):
            nc.scalar.copy(out=grouped[:].rearrange("p (c i) j -> p c j i", i=4),
                           in_=raw[:].rearrange("p j (c i) -> p c j i", i=4))

        hid_bf = sb.tile([P, Q, PACK], BF16, name="hid_bf", align_bytes=64)
        round_and_interleave(hid_bf, hid_raw)
        hid_codes = sb.tile([P, Q], U32, name="hid_codes", align_bytes=64)
        hid_plane = sb.tile([P, Q], U8, name="hid_plane", align_bytes=64)
        nc.vector.quantize_mx(out=hid_codes[:].bitcast(FP8X4), scales=hid_plane[:],
                              in_=hid_bf[:].rearrange("p q j -> p (q j)"))

        def list_slice(offsets, lo, hi):
            return offsets[:, lo // GROUP:hi // GROUP]

        word_halves = []
        for h in range(2):
            words = sb.tile([P, HALF], U32, name=f"words{h}", align_bytes=64)
            nc.vector.tensor_copy(out=words[:],
                                  in_=word_store[:].indirect(list_slice(piece_list, HALF * h, HALF * (h + 1))))
            word_halves.append(words)
        a_banks = [ps.tile([P, HALF], F32, name=f"a_bank{h}") for h in range(2)]

        def times_hid(acc, codes, plane):
            nc.tensor.matmul_mx(out=acc, lhsT=hid_codes[:].bitcast(FP8X4), lhsT_scale=hid_plane[:],
                                rhs=codes.bitcast(FP8X4), rhs_scale=plane, start=True, stop=True)

        for h, lo, hi in ((0, 0, QUARTER), (0, QUARTER, HALF), (1, 0, HALF)):
            times_hid(a_banks[h][:, lo:hi], word_halves[h][:, lo:hi], planes[:, HALF * h + lo:HALF * h + hi])

        fam_bf = sb.tile([P, U, PACK], BF16, name="fam_bf", align_bytes=64)
        round_and_interleave(fam_bf, fam_raw)
        fam_codes = sb.tile([P, U], U32, name="fam_codes", align_bytes=64)
        fam_plane = planes[4:P, :U]
        nc.vector.quantize_mx(out=fam_codes[:].bitcast(FP8X4), scales=fam_plane,
                              in_=fam_bf[:].rearrange("p u j -> p (u j)"))
        b_bank = ps.tile([P, U], F32, name="b_bank")
        times_hid(b_bank[:], fam_codes[:], fam_plane)
        nc.scalar.copy(out=b_table[:, :U], in_=b_bank[:])

        partial = fam_raw[:].rearrange("p j u -> p (j u)")
        score = sb.tile([P, I + 8], F32, name="score")
        weights = sb.tile([P, HALF + 8], F32, name="weights")
        terms = sb.tile([P, NODES], F32, name="terms")

        def add_family(lo, hi):
            nc.vector.tensor_tensor(out=score[:, lo:hi], in0=b_table[:].indirect(list_slice(family_list, lo, hi)),
                                    in1=partial[:, lo:hi], op=ALU.add)

        for h in range(2):
            cols = slice(HALF * h, HALF * (h + 1))
            nc.vector.tensor_tensor(out=partial[:, cols], in0=a_banks[h][:], in1=bias_flat[:, cols], op=ALU.add)

        add_family(0, HALF)
        neg_max0 = sb.tile([P, 1], F32, name="neg_max0")
        nc.vector.tensor_reduce(out=neg_max0[:], in_=score[:, :HALF], axis=AXIS.X, op=ALU.max, negate=True)
        total0 = sb.tile([P, 1], F32, name="total0")
        nc.scalar.activation(out=weights[:, :HALF], in_=score[:, :HALF], func=ACT.Exp, bias=neg_max0[:],
                             accum_out=total0[:])
        base0 = sb.tile([P, 1], F32, name="base0")
        nc.scalar.activation(out=base0[:], in_=neg_max0[:], func=ACT.Identity, scale=-1.0, bias=sum_one[:])
        sum0 = sb.tile([P, 1], F32, name="sum0")
        node_sum(terms, total0[:], sum0)
        nc.scalar.activation(out=score[:, I:I + 1], in_=sum0[:], func=ACT.Identity, scale=-1.0, bias=base0[:])

        add_family(HALF, HALF + QUARTER)
        add_family(HALF + QUARTER, I)
        neg_max = sb.tile([P, 1], F32, name="neg_max")
        negated = sb.tile([P, HALF], F32, name="negated")
        nc.vector.tensor_scalar(out=negated[:], in0=score[:, HALF:I], scalar1=-1.0, scalar2=neg_max0[:],
                                op0=ALU.mult, op1=ALU.min, accum_out=neg_max[:])
        total = sb.tile([P, 1], F32, name="total")
        nc.scalar.activation(out=weights[:, :HALF + 1], in_=score[:, HALF:I + 1], func=ACT.Exp, bias=neg_max[:],
                             accum_out=total[:])
        shift = sb.tile([P, 1], F32, name="shift")
        nc.vector.tensor_tensor(out=shift[:], in0=neg_max[:], in1=sum_one[:], op=ALU.subtract)
        sum_all = sb.tile([P, 1], F32, name="sum_all")
        node_sum(terms, total[:], sum_all)

        result = sb.tile([P, I], F32, name="result")
        for k in range(len(STORE_EDGES) - 1):
            cols = slice(STORE_EDGES[k], STORE_EDGES[k + 1])
            nc.vector.tensor_scalar(out=result[:, cols], in0=score[:, cols], scalar1=shift[:], scalar2=sum_all[:],
                                    op0=ALU.add, op1=ALU.add)
            (nc.sync, nc.scalar)[k % 2].dma_start(out=out[:, cols], in_=result[:, cols])
